import numpy as np
import ml_dtypes


def mxq(x, axis, fmt="e4m3"):
    dtype, down = {"e4m3": (ml_dtypes.float8_e4m3fn, 7), "e5m2": (ml_dtypes.float8_e5m2, 14)}[fmt]
    v = np.moveaxis(np.asarray(x, np.float32).astype(ml_dtypes.bfloat16).astype(np.float64), axis, -1)
    blocks = v.reshape(v.shape[:-1] + (-1, 32))
    amax = np.abs(blocks).max(-1, keepdims=True)
    byte = np.maximum(np.where(amax > 0, np.frexp(amax)[1] - 1 + 127, 0) - down, 1)
    scale = np.exp2(byte - 127.0)
    codes = (blocks / scale).astype(np.float32).astype(dtype).astype(np.float64)
    return np.moveaxis((codes * scale).reshape(v.shape), -1, axis)


WIDE = False


def mx_kscale(k):
    if not WIDE:
        return np.ones(k)
    levels = np.array([24, -24, 12, -12, 0])
    if k % 512:
        return np.exp2(np.random.permutation(np.resize(levels, k // 32))).repeat(32)
    a = np.empty((k // 512, 16))
    for p in range(k // 512):
        a[p, :8] = np.random.permutation(np.resize(levels, 8))
        for g in range(8):
            far = levels[np.abs(levels - a[p, g]) >= 10]
            a[p, g + 8] = far[np.random.randint(len(far))]
    return np.exp2(a.ravel()).repeat(32)


def f64(x):
    return np.asarray(x).astype(np.float64)


def striped8(idx):
    return np.concatenate([v.reshape(-1, 16).T for v in idx]).astype(np.uint16)


def unstriped8(offs):
    return np.stack([offs[16 * g:16 * g + 16].T.reshape(-1) for g in range(8)]).astype(np.int64)


E2M1 = np.array([0.0, 0.5, 1.0, 1.5, 2.0, 3.0, 4.0, 6.0, -0.0, -0.5, -1.0, -1.5, -2.0, -3.0, -4.0, -6.0])


def pack_weight(w, fmt):
    k, n = w.shape
    w = f64(np.asarray(w, np.float32).astype(ml_dtypes.bfloat16)).reshape(k // 32, 32, n)
    amax = np.abs(w).max(1)
    if fmt == "e4m3":
        byte = np.frexp(amax)[1] - 1 + 127 - 7
    else:
        mant, ex = np.frexp(amax / 6.0)
        byte = np.where(mant > 0.5, ex, ex - 1) + 127
    byte = np.clip(np.where(amax > 0, byte, 1), 1, 254)
    scaled = (w * np.exp2(127.0 - byte)[:, None, :]).reshape(k, n).astype(np.float32)
    by_word = np.ascontiguousarray(scaled.reshape(k // 512, 128, 4, n).transpose(0, 1, 3, 2))
    if fmt == "e4m3":
        words = by_word.astype(ml_dtypes.float8_e4m3fn).view(np.uint8)
    else:
        c = by_word.astype(ml_dtypes.float4_e2m1fn).view(np.uint8) & 0xF
        words = (c[..., 0::2] | (c[..., 1::2] << 4)).reshape(k // 512, 128, 2 * n)
    return np.ascontiguousarray(words), np.ascontiguousarray(byte.astype(np.uint8).reshape(k // 512, 16, n))


def unpack_weight(words, scales, fmt):
    g, _, n = scales.shape
    words = np.ascontiguousarray(words).reshape(g, 128, n, -1)
    if fmt == "e4m3":
        vals = words.view(ml_dtypes.float8_e4m3fn).astype(np.float64)
    else:
        nib = np.empty((g, 128, n, 4), np.uint8)
        nib[..., 0::2] = words & 0xF
        nib[..., 1::2] = words >> 4
        vals = E2M1[nib]
    vals = vals * np.repeat(np.exp2(scales.astype(np.float64) - 127.0), 8, axis=1)[..., None]
    return vals.transpose(0, 1, 3, 2).reshape(g * 512, n)


def planes(y):
    n, m = y.shape
    v = y.astype(np.float32).astype(ml_dtypes.bfloat16).astype(np.float64).reshape(n // 32, 32, m)
    top = np.abs(v).max(1)
    byte = np.clip(np.where(top > 0, np.frexp(top)[1] - 1 + 127 - 7, 1), 1, 254)
    codes = (v * np.exp2(127.0 - byte)[:, None, :]).reshape(n, m).astype(np.float32).astype(ml_dtypes.float8_e4m3fn).view(np.uint8)
    words = codes.reshape(n // 512, 128, 4, m).transpose(0, 1, 3, 2)
    return np.ascontiguousarray(words), np.ascontiguousarray(byte.astype(np.uint8).reshape(n // 512, 16, m))


K, N, T, J = 512, 512, 2048, 1024


def setup_inputs():
    n = np.random.standard_normal
    s = mx_kscale(K)[:, None]
    p_wk = pack_weight(n((K, N)) / np.sqrt(K) / s, "e4m3")
    p_wv = pack_weight(n((K, N)) / np.sqrt(K) / s, "e4m3")
    return {
        "xT": (n((K, T)) * s).astype(np.float32),
        "wgt": np.repeat(np.random.uniform(0.5, 2.0, (8, J)), 16, axis=0).astype(np.float32),
        "wk_words": p_wk[0],
        "wk_scales": p_wk[1],
        "wv_words": p_wv[0],
        "wv_scales": p_wv[1],
        "st": (n((N, J))).astype(np.float32),
        "offs": striped8(np.stack([np.random.permutation(T)[:J] for _ in range(8)])),
    }


def reference(xT, wgt, wk_words, wk_scales, wv_words, wv_scales, st, offs):
    idx = unstriped8(offs)
    rows = np.arange(K)
    xg = f64(wgt)[rows // 4 % 128] * f64(xT)[rows[:, None], idx[rows % 512 // 64]]
    xT_ = mxq(xg, 0, "e4m3")
    wk_ = unpack_weight(wk_words, wk_scales, "e4m3")
    wv_ = unpack_weight(wv_words, wv_scales, "e4m3")
    ke = wk_.T @ xT_
    ve = wv_.T @ xT_
    gate = np.tanh(ke * f64(st))
    out_0 = gate * ve
    return (out_0,) + planes(out_0)

@@ -1,0 +1,194 @@
+from contextlib import ExitStack
+
+import concourse.mybir as mybir
+
+K, N, T, J = 512, 512, 2048, 1024
+FLOPS = 2 * 2 * K * N * J
+
+F32 = mybir.dt.float32
+BF16 = mybir.dt.bfloat16
+I32 = mybir.dt.int32
+U16 = mybir.dt.uint16
+U8 = mybir.dt.uint8
+FP8X4 = mybir.dt.float8_e4m3fn_x4
+MULT = mybir.AluOpType.mult
+TANH = mybir.ActivationFunctionType.Tanh
+
+P = 128
+PACK = 4
+BANK = 512
+CHUNK = 256
+N_CHUNKS = J // CHUNK
+PIECES = (256, 256, 256, 128, 128)
+
+
+def tile_list_tanhP_kernel(
+    tc, xT, wgt, wk_words, wk_scales, wv_words, wv_scales, st, offs, out_0, out_1, out_2
+):
+    nc = tc.nc
+    chunks = [slice(c * CHUNK, (c + 1) * CHUNK) for c in range(N_CHUNKS)]
+    starts = [sum(PIECES[:u]) for u in range(len(PIECES))]
+    pieces = [slice(s, s + w) for s, w in zip(starts, PIECES)]
+
+    with ExitStack() as ctx:
+        sb = ctx.enter_context(tc.tile_pool(name="sb", bufs=1))
+        psum = ctx.enter_context(tc.psum_pool(name="psum", bufs=4))
+
+        offsets = sb.tile([P, J // 16], U16, name="offsets")
+        wgt_sb = sb.tile([P, J], F32, name="wgt_sb")
+        x_plane = [sb.tile([P, T], F32, name=f"x_plane{i}") for i in range(PACK)]
+        w_raw = [sb.tile([P, N], I32, name=f"w_raw{w}") for w in range(2)]
+        scales_raw = sb.tile([P, N], U8, name="scales_raw")
+        st_sb = [sb.tile([P, PACK, CHUNK], F32, name=f"st{c}", align_bytes=64) for c in range(N_CHUNKS)]
+        x_rows = xT.rearrange("(p i) t -> p i t", i=PACK)
+        st_rows = st.rearrange("(p t) j -> p t j", t=PACK)
+
+        def load_words(w, words):
+            nc.sync.dma_start(w_raw[w][:], words[0].rearrange("p n i -> p (n i)").bitcast(I32))
+
+        def load_scales(w, scales, queue):
+            for q in range(4):
+                first = 32 * q + 4 * w
+                queue.dma_start(
+                    scales_raw[first : first + 4, :].bitcast(I32), scales[0, 4 * q : 4 * q + 4, :].bitcast(I32)
+                )
+
+        nc.gpsimd.memset(scales_raw[:].bitcast(I32), 0)
+        load_scales(0, wk_scales, nc.gpsimd)
+        nc.sync.dma_start(offsets[:], offs)
+        nc.sync.dma_start(wgt_sb[:], wgt)
+        for i in range(PACK - 1):
+            nc.sync.dma_start(x_plane[i][:], x_rows[:, i, :])
+        load_scales(1, wv_scales, nc.sync)
+        load_words(0, wk_words)
+        nc.sync.dma_start(x_plane[PACK - 1][:], x_rows[:, PACK - 1, :])
+        load_words(1, wv_words)
+        for c, cols in enumerate(chunks):
+            nc.sync.dma_start(st_sb[c][:], st_rows[:, :, cols])
+
+        warm_in = sb.tile([P, 1], F32, name="warm_in")
+        warm_out = sb.tile([P, 1], F32, name="warm_out")
+        nc.vector.memset(warm_in[:], 0.0)
+        nc.scalar.activation(warm_out[:], warm_in[:], TANH)
+
+        xg_bf = [sb.tile([P, CHUNK, PACK], BF16, name=f"xg_bf{c}", align_bytes=64) for c in range(N_CHUNKS)]
+        xg_codes = [sb.tile([P, CHUNK], I32, name=f"xg_codes{c}", align_bytes=64) for c in range(N_CHUNKS)]
+        xg_scales = [sb.tile([P, CHUNK], U8, name=f"xg_scales{c}", align_bytes=64) for c in range(N_CHUNKS)]
+        w_scales = sb.tile([P, N], U8, name="w_scales", align_bytes=64)
+        w_codes = [sb.tile([P, N], I32, name=f"w_codes{w}", align_bytes=64) for w in range(2)]
+        y_scales = sb.tile([P, J], U8, name="y_scales", align_bytes=64)
+        out_rows = out_0.rearrange("(p t) j -> p t j", t=PACK)
+        out_words = out_1[0].rearrange("p j i -> p (j i)").bitcast(I32)
+
+        def gather(dst, i, cols):
+            window = x_plane[i][:].indirect(offsets[:, cols.start // 16 : cols.stop // 16])
+            nc.vector.tensor_tensor(dst, window, wgt_sb[:, cols], MULT)
+
+        def deal_words(w):
+            nc.vector.tensor_copy(
+                w_codes[w][:].rearrange("p (t a b) -> p a t b", t=PACK, b=4),
+                w_raw[w][:].rearrange("p (a b t) -> p a t b", t=PACK, b=4),
+            )
+
+        def high_tile(c, tag):
+            return sb.tile([P, 2, CHUNK], F32, name=f"high{c}", tag=tag, align_bytes=64)
+
+        def finish_x(c, high):
+            gather(high[:, 1, :], 3, chunks[c])
+            nc.scalar.copy(xg_bf[c][:, :, 2:4], high[:].rearrange("p i j -> p j i"))
+
+        def quantise_x(c):
+            nc.vector.quantize_mx(
+                xg_codes[c][:].bitcast(FP8X4), xg_scales[c][:], xg_bf[c][:].rearrange("p j i -> p (j i)")
+            )
+
+        def product(w, cols, slices):
+            c = cols.start // CHUNK
+            inside = slice(cols.start - c * CHUNK, cols.stop - c * CHUNK)
+            bank = psum.tile([P, len(slices), cols.stop - cols.start], F32, name=("ke", "ve")[w])
+            for s, t in enumerate(slices):
+                rows = slice(t * P, (t + 1) * P)
+                nc.tensor.matmul_mx(
+                    bank[:, s, :],
+                    lhsT=w_codes[w][:, rows].bitcast(FP8X4),
+                    lhsT_scale=w_scales[4 * w : P, rows],
+                    rhs=xg_codes[c][:, inside].bitcast(FP8X4),
+                    rhs_scale=xg_scales[c][:, inside],
+                    start=True,
+                    stop=True,
+                )
+            return bank
+
+        def groups(u):
+            per_bank = BANK // PIECES[u]
+            return [range(t, t + per_bank) for t in range(0, PACK, per_bank)]
+
+        def gates(u):
+            cols = pieces[u]
+            c = cols.start // CHUNK
+            inside = slice(cols.start - c * CHUNK, cols.stop - c * CHUNK)
+            made = []
+            for g, slices in enumerate(groups(u)):
+                ke = product(0, cols, slices)
+                arg = sb.tile([P, len(slices), PIECES[u]], F32, name=f"arg{u}_{g}")
+                nc.vector.tensor_tensor(arg[:], ke[:], st_sb[c][:, slices.start : slices.stop, inside], MULT)
+                gate = sb.tile([P, len(slices), PIECES[u]], F32, name=f"gate{u}_{g}")
+                nc.scalar.activation(gate[:], arg[:], TANH)
+                made.append(gate)
+            return made
+
+        def results(u, gate):
+            y = sb.tile([P, PACK, PIECES[u]], F32, name=f"y{u}")
+            for g, slices in enumerate(groups(u)):
+                ve = product(1, pieces[u], slices)
+                nc.vector.tensor_tensor(y[:, slices.start : slices.stop, :], ve[:], gate[g][:], MULT)
+            nc.sync.dma_start(out_rows[:, :, pieces[u]], y[:])
+            y_bf = sb.tile([P, PIECES[u], PACK], BF16, name=f"y_bf{u}", align_bytes=64)
+            nc.scalar.copy(
+                y_bf[:].rearrange("p (a b) t -> p a t b", b=4), y[:].rearrange("p t (a b) -> p a t b", b=4)
+            )
+            return y_bf
+
+        def quantise_y(u, y_bf):
+            y_codes = sb.tile([P, PIECES[u]], I32, name=f"y_codes{u}", align_bytes=64)
+            nc.vector.quantize_mx(
+                y_codes[:].bitcast(FP8X4), y_scales[:, pieces[u]], y_bf[:].rearrange("p j i -> p (j i)")
+            )
+            nc.sync.dma_start(out_words[:, pieces[u]], y_codes[:])
+
+        low = sb.tile([P, 2, J], F32, name="low")
+        for i in range(2):
+            gather(low[:, i, :], i, slice(0, J))
+        for c, cols in enumerate(chunks):
+            nc.scalar.copy(xg_bf[c][:, :, 0:2], low[:, :, cols].rearrange("p i j -> p j i"))
+        high = [high_tile(c, f"high{c}") for c in range(2)]
+        for c in range(2):
+            gather(high[c][:, 0, :], 2, chunks[c])
+        nc.vector.tensor_copy(
+            w_scales[:].rearrange("p (t m) -> p t m", t=PACK), scales_raw[:].rearrange("p (m t) -> p t m", t=PACK)
+        )
+        deal_words(0)
+        for c in range(2):
+            finish_x(c, high[c])
+        deal_words(1)
+        quantise_x(0)
+        late = high_tile(2, "xg_bf0")
+        gather(late[:, 0, :], 2, chunks[2])
+        finish_x(2, late)
+
+        y_bf = None
+        for u in range(len(PIECES)):
+            gate = gates(u)
+            if u + 1 < N_CHUNKS:
+                quantise_x(u + 1)
+            if u == 0:
+                late = high_tile(3, "st0")
+                gather(late[:, 0, :], 2, chunks[3])
+                finish_x(3, late)
+            if u > 0:
+                quantise_y(u - 1, y_bf)
+            y_bf = results(u, gate)
+        quantise_y(len(PIECES) - 1, y_bf)
+        for q in range(4):
+            queue = nc.sync if q % 2 else nc.scalar
+            queue.dma_start(out_2[0, 4 * q : 4 * q + 4, :].bitcast(I32), y_scales[32 * q : 32 * q + 4, :].bitcast(I32))

@@ -55,14 +55,17 @@ def tile_list_tanhP_kernel(
 
         nc.gpsimd.memset(scales_raw[:].bitcast(I32), 0)
         load_scales(0, wk_scales, nc.gpsimd)
+        head, rest = slice(0, CHUNK), slice(CHUNK, J)
+        nc.sync.dma_start(x_plane[0][:], x_rows[:, 0, :])
         nc.sync.dma_start(offsets[:], offs)
-        nc.sync.dma_start(wgt_sb[:], wgt)
-        for i in range(PACK - 1):
-            nc.sync.dma_start(x_plane[i][:], x_rows[:, i, :])
-        load_scales(1, wv_scales, nc.sync)
+        nc.sync.dma_start(wgt_sb[:, head], wgt[:, head])
+        nc.sync.dma_start(wgt_sb[:, rest], wgt[:, rest])
+        nc.sync.dma_start(x_plane[1][:], x_rows[:, 1, :])
         load_words(0, wk_words)
-        nc.sync.dma_start(x_plane[PACK - 1][:], x_rows[:, PACK - 1, :])
         load_words(1, wv_words)
+        nc.sync.dma_start(x_plane[2][:], x_rows[:, 2, :])
+        load_scales(1, wv_scales, nc.sync)
+        nc.sync.dma_start(x_plane[3][:], x_rows[:, 3, :])
         for c, cols in enumerate(chunks):
             nc.sync.dma_start(st_sb[c][:], st_rows[:, :, cols])
 
@@ -157,38 +160,36 @@ def tile_list_tanhP_kernel(
             nc.sync.dma_start(out_words[:, pieces[u]], y_codes[:])
 
         low = sb.tile([P, 2, J], F32, name="low")
-        for i in range(2):
-            gather(low[:, i, :], i, slice(0, J))
+        gather(low[:, 0, head], 0, head)
+        gather(low[:, 0, rest], 0, rest)
+        gather(low[:, 1, :], 1, slice(0, J))
         for c, cols in enumerate(chunks):
             nc.scalar.copy(xg_bf[c][:, :, 0:2], low[:, :, cols].rearrange("p i j -> p j i"))
-        high = [high_tile(c, f"high{c}") for c in range(2)]
-        for c in range(2):
+        deal_words(0)
+        deal_words(1)
+        high = [high_tile(c, f"high{c}") for c in range(N_CHUNKS)]
+        for c in range(N_CHUNKS):
             gather(high[c][:, 0, :], 2, chunks[c])
         nc.vector.tensor_copy(
             w_scales[:].rearrange("p (t m) -> p t m", t=PACK), scales_raw[:].rearrange("p (m t) -> p t m", t=PACK)
         )
-        deal_words(0)
-        for c in range(2):
+        for c in range(N_CHUNKS):
             finish_x(c, high[c])
-        deal_words(1)
         quantise_x(0)
-        late = high_tile(2, "xg_bf0")
-        gather(late[:, 0, :], 2, chunks[2])
-        finish_x(2, late)
+        quantise_x(1)
 
-        y_bf = None
+        last = len(PIECES) - 1
+        gate = {0: gates(0)}
+        y_bf = {}
         for u in range(len(PIECES)):
-            gate = gates(u)
-            if u + 1 < N_CHUNKS:
-                quantise_x(u + 1)
-            if u == 0:
-                late = high_tile(3, "st0")
-                gather(late[:, 0, :], 2, chunks[3])
-                finish_x(3, late)
+            if u < last:
+                gate[u + 1] = gates(u + 1)
+            if u + 2 < N_CHUNKS:
+                quantise_x(u + 2)
+            y_bf[u] = results(u, gate[u])
             if u > 0:
-                quantise_y(u - 1, y_bf)
-            y_bf = results(u, gate)
-        quantise_y(len(PIECES) - 1, y_bf)
+                quantise_y(u - 1, y_bf[u - 1])
+        quantise_y(last, y_bf[last])
         for q in range(4):
             queue = nc.sync if q % 2 else nc.scalar
             queue.dma_start(out_2[0, 4 * q : 4 * q + 4, :].bitcast(I32), y_scales[32 * q : 32 * q + 4, :].bitcast(I32))

@@ -12,6 +12,7 @@ U16 = mybir.dt.uint16
 U8 = mybir.dt.uint8
 FP8X4 = mybir.dt.float8_e4m3fn_x4
 MULT = mybir.AluOpType.mult
+ADD = mybir.AluOpType.add
 TANH = mybir.ActivationFunctionType.Tanh
 
 P = 128
@@ -61,11 +62,11 @@ def tile_list_tanhP_kernel(
         nc.sync.dma_start(wgt_sb[:, head], wgt[:, head])
         nc.sync.dma_start(wgt_sb[:, rest], wgt[:, rest])
         nc.sync.dma_start(x_plane[1][:], x_rows[:, 1, :])
-        load_words(0, wk_words)
-        load_words(1, wv_words)
         nc.sync.dma_start(x_plane[2][:], x_rows[:, 2, :])
         load_scales(1, wv_scales, nc.sync)
         nc.sync.dma_start(x_plane[3][:], x_rows[:, 3, :])
+        load_words(0, wk_words)
+        load_words(1, wv_words)
         for c, cols in enumerate(chunks):
             nc.sync.dma_start(st_sb[c][:], st_rows[:, :, cols])
 
@@ -147,9 +148,12 @@ def tile_list_tanhP_kernel(
                 nc.vector.tensor_tensor(y[:, slices.start : slices.stop, :], ve[:], gate[g][:], MULT)
             nc.sync.dma_start(out_rows[:, :, pieces[u]], y[:])
             y_bf = sb.tile([P, PIECES[u], PACK], BF16, name=f"y_bf{u}", align_bytes=64)
-            nc.scalar.copy(
-                y_bf[:].rearrange("p (a b) t -> p a t b", b=4), y[:].rearrange("p t (a b) -> p a t b", b=4)
-            )
+            if u < 2:
+                nc.gpsimd.tensor_scalar(y_bf[:], y[:].rearrange("p t j -> p j t"), 1.0, 0.0, MULT, ADD)
+            else:
+                nc.scalar.copy(
+                    y_bf[:].rearrange("p (a b) t -> p a t b", b=4), y[:].rearrange("p t (a b) -> p a t b", b=4)
+                )
             return y_bf
 
         def quantise_y(u, y_bf):
@@ -165,8 +169,6 @@ def tile_list_tanhP_kernel(
         gather(low[:, 1, :], 1, slice(0, J))
         for c, cols in enumerate(chunks):
             nc.scalar.copy(xg_bf[c][:, :, 0:2], low[:, :, cols].rearrange("p i j -> p j i"))
-        deal_words(0)
-        deal_words(1)
         high = [high_tile(c, f"high{c}") for c in range(N_CHUNKS)]
         for c in range(N_CHUNKS):
             gather(high[c][:, 0, :], 2, chunks[c])
@@ -175,7 +177,9 @@ def tile_list_tanhP_kernel(
         )
         for c in range(N_CHUNKS):
             finish_x(c, high[c])
+        deal_words(0)
         quantise_x(0)
+        deal_words(1)
         quantise_x(1)
 
         last = len(PIECES) - 1

@@ -70,11 +70,6 @@ def tile_list_tanhP_kernel(
         for c, cols in enumerate(chunks):
             nc.sync.dma_start(st_sb[c][:], st_rows[:, :, cols])
 
-        warm_in = sb.tile([P, 1], F32, name="warm_in")
-        warm_out = sb.tile([P, 1], F32, name="warm_out")
-        nc.vector.memset(warm_in[:], 0.0)
-        nc.scalar.activation(warm_out[:], warm_in[:], TANH)
-
         xg_bf = [sb.tile([P, CHUNK, PACK], BF16, name=f"xg_bf{c}", align_bytes=64) for c in range(N_CHUNKS)]
         xg_codes = [sb.tile([P, CHUNK], I32, name=f"xg_codes{c}", align_bytes=64) for c in range(N_CHUNKS)]
         xg_scales = [sb.tile([P, CHUNK], U8, name=f"xg_scales{c}", align_bytes=64) for c in range(N_CHUNKS)]

from contextlib import ExitStack

import concourse.mybir as mybir

K, N, T, J = 512, 512, 2048, 1024
FLOPS = 2 * 2 * K * N * J

F32 = mybir.dt.float32
BF16 = mybir.dt.bfloat16
I32 = mybir.dt.int32
U16 = mybir.dt.uint16
U8 = mybir.dt.uint8
FP8X4 = mybir.dt.float8_e4m3fn_x4
MULT = mybir.AluOpType.mult
ADD = mybir.AluOpType.add
TANH = mybir.ActivationFunctionType.Tanh

P = 128
PACK = 4
BANK = 512
CHUNK = 256
N_CHUNKS = J // CHUNK
PIECES = (256, 256, 256, 128, 128)


def tile_list_tanhP_kernel(
    tc, xT, wgt, wk_words, wk_scales, wv_words, wv_scales, st, offs, out_0, out_1, out_2
):
    nc = tc.nc
    chunks = [slice(c * CHUNK, (c + 1) * CHUNK) for c in range(N_CHUNKS)]
    starts = [sum(PIECES[:u]) for u in range(len(PIECES))]
    pieces = [slice(s, s + w) for s, w in zip(starts, PIECES)]

    with ExitStack() as ctx:
        sb = ctx.enter_context(tc.tile_pool(name="sb", bufs=1))
        psum = ctx.enter_context(tc.psum_pool(name="psum", bufs=4))

        offsets = sb.tile([P, J // 16], U16, name="offsets")
        wgt_sb = sb.tile([P, J], F32, name="wgt_sb")
        x_plane = [sb.tile([P, T], F32, name=f"x_plane{i}") for i in range(PACK)]
        w_raw = [sb.tile([P, N], I32, name=f"w_raw{w}") for w in range(2)]
        scales_raw = sb.tile([P, N], U8, name="scales_raw")
        st_sb = [sb.tile([P, PACK, CHUNK], F32, name=f"st{c}", align_bytes=64) for c in range(N_CHUNKS)]
        x_rows = xT.rearrange("(p i) t -> p i t", i=PACK)
        st_rows = st.rearrange("(p t) j -> p t j", t=PACK)

        def load_words(w, words):
            nc.sync.dma_start(w_raw[w][:], words[0].rearrange("p n i -> p (n i)").bitcast(I32))

        def load_scales(w, scales, queue):
            for q in range(4):
                first = 32 * q + 4 * w
                queue.dma_start(
                    scales_raw[first : first + 4, :].bitcast(I32), scales[0, 4 * q : 4 * q + 4, :].bitcast(I32)
                )

        nc.gpsimd.memset(scales_raw[:].bitcast(I32), 0)
        load_scales(0, wk_scales, nc.gpsimd)
        head, rest = slice(0, CHUNK), slice(CHUNK, J)
        nc.sync.dma_start(x_plane[0][:], x_rows[:, 0, :])
        nc.sync.dma_start(offsets[:], offs)
        nc.sync.dma_start(wgt_sb[:, head], wgt[:, head])
        nc.sync.dma_start(wgt_sb[:, rest], wgt[:, rest])
        nc.sync.dma_start(x_plane[1][:], x_rows[:, 1, :])
        nc.sync.dma_start(x_plane[2][:], x_rows[:, 2, :])
        load_scales(1, wv_scales, nc.sync)
        nc.sync.dma_start(x_plane[3][:], x_rows[:, 3, :])
        load_words(0, wk_words)
        load_words(1, wv_words)
        for c, cols in enumerate(chunks):
            nc.sync.dma_start(st_sb[c][:], st_rows[:, :, cols])

        xg_bf = [sb.tile([P, CHUNK, PACK], BF16, name=f"xg_bf{c}", align_bytes=64) for c in range(N_CHUNKS)]
        xg_codes = [sb.tile([P, CHUNK], I32, name=f"xg_codes{c}", align_bytes=64) for c in range(N_CHUNKS)]
        xg_scales = [sb.tile([P, CHUNK], U8, name=f"xg_scales{c}", align_bytes=64) for c in range(N_CHUNKS)]
        w_scales = sb.tile([P, N], U8, name="w_scales", align_bytes=64)
        w_codes = [sb.tile([P, N], I32, name=f"w_codes{w}", align_bytes=64) for w in range(2)]
        y_scales = sb.tile([P, J], U8, name="y_scales", align_bytes=64)
        out_rows = out_0.rearrange("(p t) j -> p t j", t=PACK)
        out_words = out_1[0].rearrange("p j i -> p (j i)").bitcast(I32)

        def gather(dst, i, cols):
            window = x_plane[i][:].indirect(offsets[:, cols.start // 16 : cols.stop // 16])
            nc.vector.tensor_tensor(dst, window, wgt_sb[:, cols], MULT)

        def deal_words(w):
            nc.vector.tensor_copy(
                w_codes[w][:].rearrange("p (t a b) -> p a t b", t=PACK, b=4),
                w_raw[w][:].rearrange("p (a b t) -> p a t b", t=PACK, b=4),
            )

        def high_tile(c, tag):
            return sb.tile([P, 2, CHUNK], F32, name=f"high{c}", tag=tag, align_bytes=64)

        def finish_x(c, high):
            gather(high[:, 1, :], 3, chunks[c])
            nc.scalar.copy(xg_bf[c][:, :, 2:4], high[:].rearrange("p i j -> p j i"))

        def quantise_x(c):
            nc.vector.quantize_mx(
                xg_codes[c][:].bitcast(FP8X4), xg_scales[c][:], xg_bf[c][:].rearrange("p j i -> p (j i)")
            )

        def product(w, cols, slices):
            c = cols.start // CHUNK
            inside = slice(cols.start - c * CHUNK, cols.stop - c * CHUNK)
            bank = psum.tile([P, len(slices), cols.stop - cols.start], F32, name=("ke", "ve")[w])
            for s, t in enumerate(slices):
                rows = slice(t * P, (t + 1) * P)
                nc.tensor.matmul_mx(
                    bank[:, s, :],
                    lhsT=w_codes[w][:, rows].bitcast(FP8X4),
                    lhsT_scale=w_scales[4 * w : P, rows],
                    rhs=xg_codes[c][:, inside].bitcast(FP8X4),
                    rhs_scale=xg_scales[c][:, inside],
                    start=True,
                    stop=True,
                )
            return bank

        def groups(u):
            per_bank = BANK // PIECES[u]
            return [range(t, t + per_bank) for t in range(0, PACK, per_bank)]

        def gates(u):
            cols = pieces[u]
            c = cols.start // CHUNK
            inside = slice(cols.start - c * CHUNK, cols.stop - c * CHUNK)
            made = []
            for g, slices in enumerate(groups(u)):
                ke = product(0, cols, slices)
                arg = sb.tile([P, len(slices), PIECES[u]], F32, name=f"arg{u}_{g}")
                nc.vector.tensor_tensor(arg[:], ke[:], st_sb[c][:, slices.start : slices.stop, inside], MULT)
                gate = sb.tile([P, len(slices), PIECES[u]], F32, name=f"gate{u}_{g}")
                nc.scalar.activation(gate[:], arg[:], TANH)
                made.append(gate)
            return made

        def results(u, gate):
            y = sb.tile([P, PACK, PIECES[u]], F32, name=f"y{u}")
            for g, slices in enumerate(groups(u)):
                ve = product(1, pieces[u], slices)
                nc.vector.tensor_tensor(y[:, slices.start : slices.stop, :], ve[:], gate[g][:], MULT)
            nc.sync.dma_start(out_rows[:, :, pieces[u]], y[:])
            y_bf = sb.tile([P, PIECES[u], PACK], BF16, name=f"y_bf{u}", align_bytes=64)
            if u < 2:
                nc.gpsimd.tensor_scalar(y_bf[:], y[:].rearrange("p t j -> p j t"), 1.0, 0.0, MULT, ADD)
            else:
                nc.scalar.copy(
                    y_bf[:].rearrange("p (a b) t -> p a t b", b=4), y[:].rearrange("p t (a b) -> p a t b", b=4)
                )
            return y_bf

        def quantise_y(u, y_bf):
            y_codes = sb.tile([P, PIECES[u]], I32, name=f"y_codes{u}", align_bytes=64)
            nc.vector.quantize_mx(
                y_codes[:].bitcast(FP8X4), y_scales[:, pieces[u]], y_bf[:].rearrange("p j i -> p (j i)")
            )
            nc.sync.dma_start(out_words[:, pieces[u]], y_codes[:])

        low = sb.tile([P, 2, J], F32, name="low")
        gather(low[:, 0, head], 0, head)
        gather(low[:, 0, rest], 0, rest)
        gather(low[:, 1, :], 1, slice(0, J))
        for c, cols in enumerate(chunks):
            nc.scalar.copy(xg_bf[c][:, :, 0:2], low[:, :, cols].rearrange("p i j -> p j i"))
        high = [high_tile(c, f"high{c}") for c in range(N_CHUNKS)]
        for c in range(N_CHUNKS):
            gather(high[c][:, 0, :], 2, chunks[c])
        nc.vector.tensor_copy(
            w_scales[:].rearrange("p (t m) -> p t m", t=PACK), scales_raw[:].rearrange("p (m t) -> p t m", t=PACK)
        )
        for c in range(N_CHUNKS):
            finish_x(c, high[c])
        deal_words(0)
        quantise_x(0)
        deal_words(1)
        quantise_x(1)

        last = len(PIECES) - 1
        gate = {0: gates(0)}
        y_bf = {}
        for u in range(len(PIECES)):
            if u < last:
                gate[u + 1] = gates(u + 1)
            if u + 2 < N_CHUNKS:
                quantise_x(u + 2)
            y_bf[u] = results(u, gate[u])
            if u > 0:
                quantise_y(u - 1, y_bf[u - 1])
        quantise_y(last, y_bf[last])
        for q in range(4):
            queue = nc.sync if q % 2 else nc.scalar
            queue.dma_start(out_2[0, 4 * q : 4 * q + 4, :].bitcast(I32), y_scales[32 * q : 32 * q + 4, :].bitcast(I32))
